import numpy as np, ml_dtypes
CORES = [36,164,52,180,100,228,116,244]
N = 8
TOK, CAP, FF = 256, 48, 8
def entries(a): return a.T.reshape(-1)
def pack(v, P): return np.ascontiguousarray(np.asarray(v, np.int32).reshape(-1, P).T)
def lists(rng, how):
    E = rng.integers(0, N, (N, TOK))
    if how == "hot": E[:] = rng.integers(N)
    if how == "none": E = (int(rng.integers(N)) + 1 + rng.integers(0, N - 1, (N, TOK))) % N
    if how == "skew": E = np.where(rng.random((N, TOK)) < 0.7, rng.integers(0, N, (N, 1)), E)
    if how == "even": E = np.stack([rng.permutation(np.arange(TOK) % N) for r in range(N)])
    if how == "own": E = np.repeat(np.arange(N).reshape(N, 1), TOK, axis=1)
    return {"ex": np.stack([pack(E[r], 16) for r in range(N)]), "pos": np.stack([pack(p, 16) for p in np.stack([np.array([np.sum(E[r, :t] == E[r, t]) for t in range(TOK)]) for r in range(N)])])}
def setup_inputs(rng):
    return dict({"x": rng.standard_normal((N, 128, TOK), dtype=np.float32).astype(ml_dtypes.bfloat16), "w1": (rng.standard_normal((N, 128, FF * 128), dtype=np.float32) / 8).astype(ml_dtypes.bfloat16), "w2": (rng.standard_normal((N, 128, FF * 128), dtype=np.float32) / 16).astype(ml_dtypes.bfloat16)}, **lists(rng, "uniform"))
def setup_inputs_even(rng):
    d = setup_inputs(rng); d.update(lists(rng, "even"))
    for k in ("x",): d[k] = (d[k].astype(np.float32) * 1024.0).astype(d[k].dtype)
    return d
def setup_inputs_hot(rng):
    d = setup_inputs(rng); d.update(lists(rng, "hot"))
    for k in ("x",): d[k] = (d[k].astype(np.float32) * (1 / 1024.0)).astype(d[k].dtype)
    return d
def setup_inputs_none(rng):
    d = setup_inputs(rng); d.update(lists(rng, "none"))
    return d
def setup_inputs_own(rng):
    d = setup_inputs(rng); d.update(lists(rng, "own"))
    return d
def setup_inputs_skew(rng):
    d = setup_inputs(rng); d.update(lists(rng, "skew"))
    return d
def check_inputs(x):
    bad = []
    if x["ex"].min() < 0 or x["ex"].max() >= N: bad.append("ex out of range")
    E = np.stack([entries(a) for a in x["ex"]])
    if not np.array_equal(np.stack([entries(a) for a in x["pos"]]), np.stack([np.array([np.sum(E[r, :t] == E[r, t]) for t in range(TOK)]) for r in range(N)])): bad.append("pos isn't the place")
    return bad
def reference(x, w1, w2, ex, pos):
    X, W1, W2 = x.astype(np.float64), w1.astype(np.float64), w2.astype(np.float64)
    y = np.zeros((N, 128, TOK))
    for r in range(N):
        E = entries(ex[r]); place = np.array([np.sum(E[:t] == E[t]) for t in range(TOK)])
        for k in range(N):
            m = (E == k) & (place < CAP)
            y[r][:, m] = sum(W2[k][:, 128 * f:128 * f + 128].T @ np.maximum(W1[k][:, 128 * f:128 * f + 128].T @ X[r][:, m], 0.0) for f in range(FF))
    return {"y": y.astype(ml_dtypes.bfloat16)}

@@ -1,0 +1,243 @@
+from concourse.bass import DstId, RemoteDMATransfer
+from concourse.mybir import AluOpType, ActivationFunctionType
+
+NR, TOK, CAP, FF, D = 8, 256, 48, 8, 128
+STR = TOK
+WIN = NR * STR
+NSIM = 256
+HALF = FF * D // 2
+
+MAIN_GROUPS = [[1, 2], [3, 4], [5, 6], [7]]
+HELP_GROUPS = []
+DISPATCH = [[1, 2], [3, 4], [5, 6], [7]]
+PIECES = [(0, 3, "v"), (3, 6, "s"), (6, 8, "v")]
+GMAX = 2
+
+SCRATCH = {
+    "xs": ("sbuf", [128, TOK], "bfloat16"),
+    "exi": ("sbuf", [16, 32], "int32"),
+    "exb": ("sbuf", [16, 32], "bfloat16"),
+    "rsel": ("sbuf", [16, 256], "bfloat16"),
+    "off": ("sbuf", [128, 16], "uint16"),
+    "send": ("sbuf", [128, WIN], "bfloat16"),
+    "res": ("sbuf", [128, WIN], "bfloat16"),
+    "land": ("sbuf", [128, (NR - 1) * CAP], "bfloat16"),
+    "outb": ("sbuf", [128, (NR - 1) * CAP], "bfloat16"),
+    "hs": ("sbuf", [128, FF * GMAX * CAP], "bfloat16"),
+    "w1s": ("sbuf", [128, FF * D], "bfloat16"),
+    "w2s": ("sbuf", [128, FF * D], "bfloat16"),
+    "ys": ("sbuf", [128, TOK], "bfloat16"),
+    "p0": ("psum", [128, 512], "float32"),
+    "p1": ("psum", [128, 512], "float32"),
+    "p2": ("psum", [128, 512], "float32"),
+    "pc": ("psum", [128, 512], "float32"),
+    "po": ("psum", [128, 512], "float32"),
+}
+SEMAPHORES = ["idx", "xl", "wa", "wb", "wc", "wd", "rm", "ms", "zs", "cv", "of", "rs", "sc",
+              "a1", "a2", "a3", "a4", "a5", "a6", "a7", "m0", "m1", "m2", "r0", "r1", "r2", "mm", "cp",
+              "sent", "back", "g1", "g2", "st"]
+
+
+def _bits(mask):
+    return [1 << b for b in range(16) if (mask >> b) & 1]
+
+
+def _split(mask, n):
+    e = _bits(mask)
+    per = 1
+    while per * 2 * n <= len(e):
+        per *= 2
+    return [sum(e[i * per:(i + 1) * per]) for i in range(n)], per
+
+
+def _common(topo, src, dsts):
+    m = topo.mask(src, dsts[0])
+    for d in dsts[1:]:
+        m &= topo.mask(src, d)
+    return m
+
+
+def _post(g, topo, src, items, local_sem):
+    subs, per = _split(_common(topo, src, [it[0] for it in items]), len(items))
+    if len(items) == 1:
+        d, o, i_, s = items[0]
+        rid, pid = topo.addr(d, src)
+        g.remote_dma(out_ap=o, in_ap=i_, remote_sem=s, local_sem=local_sem, pid=pid, routing_id=rid,
+                     dma_engine_mask=subs[0])
+    else:
+        tr = []
+        for (d, o, i_, s), m in zip(items, subs):
+            rid, pid = topo.addr(d, src)
+            tr.append(RemoteDMATransfer(dst_ids=[DstId(rid=rid, pnc=pid)], dma_engine_mask=m, remote_sem=s,
+                                        src=i_, dst=o))
+        g.remote_dma_fused(tr, local_sem=local_sem)
+    return per * len(items)
+
+
+def _helper(topo, cores, m):
+    for c in range(NSIM):
+        if (c not in cores and topo.host(c) == topo.host(m) and topo.chip(c) == topo.chip(m)
+                and topo.die(c) == topo.die(m) and all(topo.may_write(c, d) for d in cores)):
+            return c
+    return None
+
+
+def _expert(g, T, groups, wcount):
+    S = T.sem
+    pe, v, sc = g.tensor, g.vector, g.scalar
+    banks = [T.p0, T.p1, T.p2]
+    for gi, (rhs, n, waits, out) in enumerate(groups):
+        for s_, val in waits:
+            pe.wait_ge(s_, val)
+        for pi, (lo, hi, q) in enumerate(PIECES):
+            for f in range(lo, hi):
+                if gi == 0 and f % 4 == 0:
+                    pe.wait_ge(S.wa if f == 0 else S.wb, wcount)
+                pe.matmul(banks[pi][:, (f - lo) * n:(f - lo + 1) * n], T.w1s[:, f * D:(f + 1) * D], rhs,
+                          True, True).then_inc(S["m%d" % pi], 1)
+        if gi > 0:
+            pe.wait_ge(S.cp, gi)
+        for pi, (lo, hi, q) in enumerate(PIECES):
+            pe.wait_ge(S["r%d" % pi], gi + 1)
+            for f in range(lo, hi):
+                if gi == 0 and f % 4 == 0:
+                    pe.wait_ge(S.wc if f == 0 else S.wd, wcount)
+                pe.matmul(T.pc[:, 0:n], T.w2s[:, f * D:(f + 1) * D], T.hs[:, f * n:(f + 1) * n],
+                          f == 0, f == FF - 1).then_inc(S.mm, 1)
+        for pi, (lo, hi, q) in enumerate(PIECES):
+            eng = v if q == "v" else sc
+            eng.wait_ge(S["m%d" % pi], (hi - lo) * (gi + 1))
+            if gi > 0:
+                eng.wait_ge(S.cp, gi)
+            w = (hi - lo) * n
+            if q == "v":
+                v.tensor_scalar(T.hs[:, lo * n:hi * n], banks[pi][:, 0:w], 0.0, None,
+                                AluOpType.max).then_inc(S["r%d" % pi], 1)
+            else:
+                sc.activation(T.hs[:, lo * n:hi * n], banks[pi][:, 0:w],
+                              ActivationFunctionType.Relu).then_inc(S["r%d" % pi], 1)
+        v.wait_ge(S.mm, FF * (gi + 1))
+        v.tensor_copy(out, T.pc[:, 0:n]).then_inc(S.cp, 1)
+
+
+def rank_program(g, core, T, topo):
+    cores = list(T.cores)
+    S = T.sem
+    rank = T.rank_of(core)
+    helpers = [_helper(topo, cores, m) for m in cores] if HELP_GROUPS else [None] * NR
+    main_steps = [j for G in MAIN_GROUPS for j in G]
+    help_steps = [j for G in HELP_GROUPS for j in G]
+
+    def owner(e, j):
+        return cores[e] if j in main_steps else helpers[e]
+
+    def landcol(j):
+        lst = main_steps if j in main_steps else help_steps
+        return lst.index(j) * CAP
+
+    def arrive(e, j):
+        r = (e - j) % NR
+        call = [c for c in DISPATCH if j in c][0]
+        return _split(_common(topo, cores[r], [owner((r + jj) % NR, jj) for jj in call]), len(call))[1]
+
+    def remote_groups(e, plan):
+        out = []
+        for G in plan:
+            c0, n = landcol(G[0]), CAP * len(G)
+            out.append((T.land[:, c0:c0 + n], n, [(S["a%d" % j], arrive(e, j)) for j in G], T.outb[:, c0:c0 + n]))
+        return out
+
+    def give_back(e, plan, first, sent):
+        for i, G in enumerate(plan):
+            g.wait_ge(S.cp, first + i + 1)
+            sent += _post(g, topo, core,
+                          [(cores[(e - j) % NR], T.res[:, e * STR:e * STR + CAP],
+                            T.outb[:, landcol(j):landcol(j) + CAP], S.back) for j in G], S.sent)
+        return sent
+
+    if rank is None:
+        if core not in helpers:
+            return
+        e = helpers.index(core)
+        fm = topo.mask(cores[e], core) & ~topo.mask(cores[e], cores[(e + 1) % NR])
+        _expert(g, T, remote_groups(e, HELP_GROUPS), len(_bits(fm)))
+        g.wait_ge(S.sent, give_back(e, HELP_GROUPS, 0, 0))
+        return
+
+    k = rank
+    v, sc, pe, sy = g.vector, g.scalar, g.tensor, g.sync
+
+    sy.dma_start(T.exi[:, 0:16], T.ex[:]).then_inc(S.idx, 16)
+    sc.dma_start(T.exi[:, 16:32], T.pos[:]).then_inc(S.idx, 16)
+    sy.dma_start(T.xs[:], T.x[:]).then_inc(S.xl, 16)
+    sc.dma_start(T.w1s[:, 0:HALF], T.w1[:, 0:HALF]).then_inc(S.wa, 16)
+    sy.dma_start(T.w1s[:, HALF:2 * HALF], T.w1[:, HALF:2 * HALF]).then_inc(S.wb, 16)
+    sc.dma_start(T.w2s[:, 0:HALF], T.w2[:, 0:HALF]).then_inc(S.wc, 16)
+    sy.dma_start(T.w2s[:, HALF:2 * HALF], T.w2[:, HALF:2 * HALF]).then_inc(S.wd, 16)
+
+    v.memset(T.rsel[:, 0:128], float(STR)).then_inc(S.rm, 1)
+    v.memset(T.rsel[:, 128:256], 1.0).then_inc(S.rm, 1)
+    for e in range(NR):
+        v.memset(T.send[:, e * STR:e * STR + CAP], 0.0).then_inc(S.ms, 1)
+    g.wait_ge(S.rm, 2)
+    g.affine_select(T.rsel[:], T.rsel[:], [[0, 16], [-1, 16]], AluOpType.is_equal, 0.0, 0, 1).then_inc(S.rs, 1)
+
+    v.wait_ge(S.idx, 32)
+    v.tensor_copy(T.exb[:], T.exi[:]).then_inc(S.cv, 1)
+    pe.wait_ge(S.cv, 1)
+    pe.wait_ge(S.rs, 1)
+    pe.matmul(T.po[:, 0:16], T.rsel[:, 0:128], T.exb[:, 0:16], True, False).then_inc(S.of, 1)
+    pe.matmul(T.po[:, 0:16], T.rsel[:, 128:256], T.exb[:, 16:32], False, True).then_inc(S.of, 1)
+    v.wait_ge(S.of, 2)
+    v.tensor_copy(T.off[:], T.po[:, 0:16]).then_inc(S.cv, 1)
+
+    v.wait_ge(S.cv, 2)
+    v.wait_ge(S.xl, 16)
+    v.wait_ge(S.ms, NR)
+    v.tensor_copy(T.send[:, 0:WIN].indirect(T.off[:, 0:16]), T.xs[:]).then_inc(S.sc, 1)
+    for e in range(NR):
+        v.memset(T.res[:, e * STR + CAP:(e + 1) * STR], 0.0).then_inc(S.zs, 1)
+
+    g.wait_ge(S.sc, 1)
+    sent = 0
+    for call in DISPATCH:
+        sent += _post(g, topo, core,
+                      [(owner((k + j) % NR, j), T.land[:, landcol(j):landcol(j) + CAP],
+                        T.send[:, ((k + j) % NR) * STR:((k + j) % NR) * STR + CAP], S["a%d" % j]) for j in call],
+                      S.sent)
+
+    if HELP_GROUPS:
+        h = helpers[k]
+        fm = topo.mask(core, h) & ~topo.mask(core, cores[(k + 1) % NR])
+        rid, pid = topo.addr(h, core)
+        for buf, lo, s_ in ((T.w1s, 0, S.wa), (T.w1s, HALF, S.wb), (T.w2s, 0, S.wc), (T.w2s, HALF, S.wd)):
+            g.wait_ge(s_, 16)
+            g.remote_dma(out_ap=buf[:, lo:lo + HALF], in_ap=buf[:, lo:lo + HALF], remote_sem=s_, local_sem=S.sent,
+                         pid=pid, routing_id=rid, dma_engine_mask=fm)
+            sent += len(_bits(fm))
+
+    own = (T.send[:, k * STR:k * STR + CAP], CAP, [(S.sc, 1)], T.res[:, k * STR:k * STR + CAP])
+    groups = [own] + remote_groups(k, MAIN_GROUPS)
+    _expert(g, T, groups, 16)
+    sent = give_back(k, MAIN_GROUPS, 1, sent)
+    g.wait_ge(S.sent, sent)
+
+    back = 0
+    for j in range(1, NR):
+        e = (k + j) % NR
+        G = [G for G in MAIN_GROUPS + HELP_GROUPS if j in G][0]
+        back += _split(_common(topo, owner(e, j), [cores[(e - jj) % NR] for jj in G]), len(G))[1]
+    for eng in (v, sc):
+        eng.wait_ge(S.back, back)
+        eng.wait_ge(S.zs, NR)
+        eng.wait_ge(S.cp, len(groups))
+        eng.wait_ge(S.cv, 2)
+    h2 = TOK // 2
+    v.tensor_copy(T.ys[:, 0:h2], T.res[:, 0:WIN].indirect(T.off[:, 0:8])).then_inc(S.g1, 1)
+    sc.activation(T.ys[:, h2:TOK], T.res[:, 0:WIN].indirect(T.off[:, 8:16]),
+                  ActivationFunctionType.Copy).then_inc(S.g2, 1)
+    sy.wait_ge(S.g1, 1)
+    sy.dma_start(T.y[:, 0:h2], T.ys[:, 0:h2]).then_inc(S.st, 16)
+    sc.wait_ge(S.g2, 1)
+    sc.dma_start(T.y[:, h2:TOK], T.ys[:, h2:TOK]).then_inc(S.st, 16)
+    sy.wait_ge(S.st, 32)

@@ -7,8 +7,8 @@ WIN = NR * STR
 NSIM = 256
 HALF = FF * D // 2
 
-MAIN_GROUPS = [[1, 2], [3, 4], [5, 6], [7]]
-HELP_GROUPS = []
+MAIN_GROUPS = [[1, 2], [5, 6]]
+HELP_GROUPS = [[3, 4], [7]]
 DISPATCH = [[1, 2], [3, 4], [5, 6], [7]]
 PIECES = [(0, 3, "v"), (3, 6, "s"), (6, 8, "v")]
 GMAX = 2

@@ -5,13 +5,14 @@ NR, TOK, CAP, FF, D = 8, 256, 48, 8, 128
 STR = TOK
 WIN = NR * STR
 NSIM = 256
-HALF = FF * D // 2
 
-MAIN_GROUPS = [[1, 2], [5, 6]]
-HELP_GROUPS = [[3, 4], [7]]
-DISPATCH = [[1, 2], [3, 4], [5, 6], [7]]
+MAIN_GROUPS = [[1, 2], [5], [7]]
+HELP_GROUPS = [[3, 4], [6]]
+DISPATCH = [[1, 2], [3, 4], [5], [6], [7]]
 PIECES = [(0, 3, "v"), (3, 6, "s"), (6, 8, "v")]
 GMAX = 2
+CHUNKS = [(1, 0, 1, "w0", "s", True), (1, 1, 4, "wa", "s", False), (1, 4, 8, "wb", "y", False),
+          (2, 0, 4, "wc", "s", False), (2, 4, 8, "wd", "y", False)]
 
 SCRATCH = {
     "xs": ("sbuf", [128, TOK], "bfloat16"),
@@ -33,7 +34,7 @@ SCRATCH = {
     "pc": ("psum", [128, 512], "float32"),
     "po": ("psum", [128, 512], "float32"),
 }
-SEMAPHORES = ["idx", "xl", "wa", "wb", "wc", "wd", "rm", "ms", "zs", "cv", "of", "rs", "sc",
+SEMAPHORES = ["idx", "xl", "w0", "wa", "wb", "wc", "wd", "rm", "ms", "zs", "cv", "of", "rs", "sc",
               "a1", "a2", "a3", "a4", "a5", "a6", "a7", "m0", "m1", "m2", "r0", "r1", "r2", "mm", "cp",
               "sent", "back", "g1", "g2", "st"]
 
@@ -82,7 +83,7 @@ def _helper(topo, cores, m):
     return None
 
 
-def _expert(g, T, groups, wcount):
+def _expert(g, T, groups, wneed):
     S = T.sem
     pe, v, sc = g.tensor, g.vector, g.scalar
     banks = [T.p0, T.p1, T.p2]
@@ -91,8 +92,8 @@ def _expert(g, T, groups, wcount):
             pe.wait_ge(s_, val)
         for pi, (lo, hi, q) in enumerate(PIECES):
             for f in range(lo, hi):
-                if gi == 0 and f % 4 == 0:
-                    pe.wait_ge(S.wa if f == 0 else S.wb, wcount)
+                if gi == 0 and (1, f) in wneed:
+                    pe.wait_ge(*wneed[(1, f)])
                 pe.matmul(banks[pi][:, (f - lo) * n:(f - lo + 1) * n], T.w1s[:, f * D:(f + 1) * D], rhs,
                           True, True).then_inc(S["m%d" % pi], 1)
         if gi > 0:
@@ -100,8 +101,8 @@ def _expert(g, T, groups, wcount):
         for pi, (lo, hi, q) in enumerate(PIECES):
             pe.wait_ge(S["r%d" % pi], gi + 1)
             for f in range(lo, hi):
-                if gi == 0 and f % 4 == 0:
-                    pe.wait_ge(S.wc if f == 0 else S.wd, wcount)
+                if gi == 0 and (2, f) in wneed:
+                    pe.wait_ge(*wneed[(2, f)])
                 pe.matmul(T.pc[:, 0:n], T.w2s[:, f * D:(f + 1) * D], T.hs[:, f * n:(f + 1) * n],
                           f == 0, f == FF - 1).then_inc(S.mm, 1)
         for pi, (lo, hi, q) in enumerate(PIECES):
@@ -155,12 +156,16 @@ def rank_program(g, core, T, topo):
                             T.outb[:, landcol(j):landcol(j) + CAP], S.back) for j in G], S.sent)
         return sent
 
+    def pass_mask(e, early):
+        far = topo.mask(cores[e], cores[(e + 1) % NR])
+        return topo.mask(cores[e], helpers[e]) & (far if early else ~far)
+
     if rank is None:
         if core not in helpers:
             return
         e = helpers.index(core)
-        fm = topo.mask(cores[e], core) & ~topo.mask(cores[e], cores[(e + 1) % NR])
-        _expert(g, T, remote_groups(e, HELP_GROUPS), len(_bits(fm)))
+        wneed = dict(((l, lo), (S[s_], len(_bits(pass_mask(e, early))))) for l, lo, hi, s_, q, early in CHUNKS)
+        _expert(g, T, remote_groups(e, HELP_GROUPS), wneed)
         g.wait_ge(S.sent, give_back(e, HELP_GROUPS, 0, 0))
         return
 
@@ -170,10 +175,9 @@ def rank_program(g, core, T, topo):
     sy.dma_start(T.exi[:, 0:16], T.ex[:]).then_inc(S.idx, 16)
     sc.dma_start(T.exi[:, 16:32], T.pos[:]).then_inc(S.idx, 16)
     sy.dma_start(T.xs[:], T.x[:]).then_inc(S.xl, 16)
-    sc.dma_start(T.w1s[:, 0:HALF], T.w1[:, 0:HALF]).then_inc(S.wa, 16)
-    sy.dma_start(T.w1s[:, HALF:2 * HALF], T.w1[:, HALF:2 * HALF]).then_inc(S.wb, 16)
-    sc.dma_start(T.w2s[:, 0:HALF], T.w2[:, 0:HALF]).then_inc(S.wc, 16)
-    sy.dma_start(T.w2s[:, HALF:2 * HALF], T.w2[:, HALF:2 * HALF]).then_inc(S.wd, 16)
+    for l, lo, hi, s_, q, early in CHUNKS:
+        buf, src = (T.w1s, T.w1) if l == 1 else (T.w2s, T.w2)
+        (sc if q == "s" else sy).dma_start(buf[:, lo * D:hi * D], src[:, lo * D:hi * D]).then_inc(S[s_], 16)
 
     v.memset(T.rsel[:, 0:128], float(STR)).then_inc(S.rm, 1)
     v.memset(T.rsel[:, 128:256], 1.0).then_inc(S.rm, 1)
@@ -198,27 +202,37 @@ def rank_program(g, core, T, topo):
     for e in range(NR):
         v.memset(T.res[:, e * STR + CAP:(e + 1) * STR], 0.0).then_inc(S.zs, 1)
 
-    g.wait_ge(S.sc, 1)
     sent = 0
+
+    def pass_on(when, sent):
+        if not HELP_GROUPS:
+            return sent
+        rid, pid = topo.addr(helpers[k], core)
+        for l, lo, hi, s_, q, early in CHUNKS:
+            if early != when:
+                continue
+            buf = T.w1s if l == 1 else T.w2s
+            fm = pass_mask(k, early)
+            g.wait_ge(S[s_], 16)
+            g.remote_dma(out_ap=buf[:, lo * D:hi * D], in_ap=buf[:, lo * D:hi * D], remote_sem=S[s_],
+                         local_sem=S.sent, pid=pid, routing_id=rid, dma_engine_mask=fm)
+            sent += len(_bits(fm))
+        return sent
+
+    sent = pass_on(True, sent)
+
+    g.wait_ge(S.sc, 1)
     for call in DISPATCH:
         sent += _post(g, topo, core,
                       [(owner((k + j) % NR, j), T.land[:, landcol(j):landcol(j) + CAP],
                         T.send[:, ((k + j) % NR) * STR:((k + j) % NR) * STR + CAP], S["a%d" % j]) for j in call],
                       S.sent)
 
-    if HELP_GROUPS:
-        h = helpers[k]
-        fm = topo.mask(core, h) & ~topo.mask(core, cores[(k + 1) % NR])
-        rid, pid = topo.addr(h, core)
-        for buf, lo, s_ in ((T.w1s, 0, S.wa), (T.w1s, HALF, S.wb), (T.w2s, 0, S.wc), (T.w2s, HALF, S.wd)):
-            g.wait_ge(s_, 16)
-            g.remote_dma(out_ap=buf[:, lo:lo + HALF], in_ap=buf[:, lo:lo + HALF], remote_sem=s_, local_sem=S.sent,
-                         pid=pid, routing_id=rid, dma_engine_mask=fm)
-            sent += len(_bits(fm))
+    sent = pass_on(False, sent)
 
     own = (T.send[:, k * STR:k * STR + CAP], CAP, [(S.sc, 1)], T.res[:, k * STR:k * STR + CAP])
     groups = [own] + remote_groups(k, MAIN_GROUPS)
-    _expert(g, T, groups, 16)
+    _expert(g, T, groups, dict(((l, lo), (S[s_], 16)) for l, lo, hi, s_, q, early in CHUNKS))
     sent = give_back(k, MAIN_GROUPS, 1, sent)
     g.wait_ge(S.sent, sent)
 

@@ -6,13 +6,12 @@ STR = TOK
 WIN = NR * STR
 NSIM = 256
 
-MAIN_GROUPS = [[1, 2], [5], [7]]
-HELP_GROUPS = [[3, 4], [6]]
+PLAN = [[[1, 2], [5]], [[3, 4], [6]], [[7]]]
 DISPATCH = [[1, 2], [3, 4], [5], [6], [7]]
 PIECES = [(0, 3, "v"), (3, 6, "s"), (6, 8, "v")]
 GMAX = 2
-CHUNKS = [(1, 0, 1, "w0", "s", True), (1, 1, 4, "wa", "s", False), (1, 4, 8, "wb", "y", False),
-          (2, 0, 4, "wc", "s", False), (2, 4, 8, "wd", "y", False)]
+CHUNKS = [(1, 0, 1, "w0", "s", True, "far"), (1, 1, 4, "wa", "s", False, "near"), (1, 4, 8, "wb", "y", False, "near"),
+          (2, 0, 4, "wc", "s", False, "far"), (2, 4, 6, "wd", "y", False, "near"), (2, 6, 8, "we", "y", False, "near")]
 
 SCRATCH = {
     "xs": ("sbuf", [128, TOK], "bfloat16"),
@@ -25,18 +24,23 @@ SCRATCH = {
     "land": ("sbuf", [128, (NR - 1) * CAP], "bfloat16"),
     "outb": ("sbuf", [128, (NR - 1) * CAP], "bfloat16"),
     "hs": ("sbuf", [128, FF * GMAX * CAP], "bfloat16"),
+    "hs2": ("sbuf", [128, FF * GMAX * CAP], "bfloat16"),
     "w1s": ("sbuf", [128, FF * D], "bfloat16"),
     "w2s": ("sbuf", [128, FF * D], "bfloat16"),
     "ys": ("sbuf", [128, TOK], "bfloat16"),
+    "zb": ("sbuf", [128, STR - CAP], "bfloat16"),
     "p0": ("psum", [128, 512], "float32"),
     "p1": ("psum", [128, 512], "float32"),
     "p2": ("psum", [128, 512], "float32"),
+    "q0": ("psum", [128, 512], "float32"),
+    "q1": ("psum", [128, 512], "float32"),
+    "q2": ("psum", [128, 512], "float32"),
     "pc": ("psum", [128, 512], "float32"),
     "po": ("psum", [128, 512], "float32"),
 }
-SEMAPHORES = ["idx", "xl", "w0", "wa", "wb", "wc", "wd", "rm", "ms", "zs", "cv", "of", "rs", "sc",
-              "a1", "a2", "a3", "a4", "a5", "a6", "a7", "m0", "m1", "m2", "r0", "r1", "r2", "mm", "cp",
-              "sent", "back", "g1", "g2", "st"]
+SEMAPHORES = ["idx", "xl", "w0", "wa", "wb", "wc", "wd", "we", "rm", "ms", "zs", "cv", "of", "rs", "sc",
+              "a1", "a2", "a3", "a4", "a5", "a6", "a7", "m0", "m1", "m2", "r0", "r1", "r2",
+              "n0", "n1", "n2", "u0", "u1", "u2", "mm", "cp", "sent", "back", "g1", "g2", "st"]
 
 
 def _bits(mask):
@@ -75,66 +79,88 @@ def _post(g, topo, src, items, local_sem):
     return per * len(items)
 
 
-def _helper(topo, cores, m):
-    for c in range(NSIM):
-        if (c not in cores and topo.host(c) == topo.host(m) and topo.chip(c) == topo.chip(m)
-                and topo.die(c) == topo.die(m) and all(topo.may_write(c, d) for d in cores)):
-            return c
-    return None
+def _team(topo, cores, m):
+    more = [c for c in range(NSIM)
+            if (c not in cores and topo.host(c) == topo.host(m) and topo.chip(c) == topo.chip(m)
+                and topo.die(c) == topo.die(m) and all(topo.may_write(c, d) for d in cores))]
+    return [m] + more[:len(PLAN) - 1]
 
 
 def _expert(g, T, groups, wneed):
     S = T.sem
     pe, v, sc = g.tensor, g.vector, g.scalar
-    banks = [T.p0, T.p1, T.p2]
-    for gi, (rhs, n, waits, out) in enumerate(groups):
+    banks = [[T.p0, T.p1, T.p2], [T.q0, T.q1, T.q2]]
+    hid = [T.hs, T.hs2]
+
+    def msem(gi, pi):
+        return S["%s%d" % ("mn"[gi % 2], pi)]
+
+    def rsem(gi, pi):
+        return S["%s%d" % ("ru"[gi % 2], pi)]
+
+    def layer1(gi):
+        rhs, n, waits, out = groups[gi]
         for s_, val in waits:
             pe.wait_ge(s_, val)
         for pi, (lo, hi, q) in enumerate(PIECES):
             for f in range(lo, hi):
                 if gi == 0 and (1, f) in wneed:
                     pe.wait_ge(*wneed[(1, f)])
-                pe.matmul(banks[pi][:, (f - lo) * n:(f - lo + 1) * n], T.w1s[:, f * D:(f + 1) * D], rhs,
-                          True, True).then_inc(S["m%d" % pi], 1)
+                pe.matmul(banks[gi % 2][pi][:, (f - lo) * n:(f - lo + 1) * n], T.w1s[:, f * D:(f + 1) * D], rhs,
+                          True, True).then_inc(msem(gi, pi), 1)
+        for pi, (lo, hi, q) in enumerate(PIECES):
+            eng = v if q == "v" else sc
+            eng.wait_ge(msem(gi, pi), (hi - lo) * (gi // 2 + 1))
+            if gi > 1:
+                eng.wait_ge(S.cp, gi - 1)
+            w = (hi - lo) * n
+            if q == "v":
+                v.tensor_scalar(hid[gi % 2][:, lo * n:hi * n], banks[gi % 2][pi][:, 0:w], 0.0, None,
+                                AluOpType.max).then_inc(rsem(gi, pi), 1)
+            else:
+                sc.activation(hid[gi % 2][:, lo * n:hi * n], banks[gi % 2][pi][:, 0:w],
+                              ActivationFunctionType.Relu).then_inc(rsem(gi, pi), 1)
+
+    def layer2(gi):
+        rhs, n, waits, out = groups[gi]
         if gi > 0:
             pe.wait_ge(S.cp, gi)
         for pi, (lo, hi, q) in enumerate(PIECES):
-            pe.wait_ge(S["r%d" % pi], gi + 1)
+            pe.wait_ge(rsem(gi, pi), gi // 2 + 1)
             for f in range(lo, hi):
                 if gi == 0 and (2, f) in wneed:
                     pe.wait_ge(*wneed[(2, f)])
-                pe.matmul(T.pc[:, 0:n], T.w2s[:, f * D:(f + 1) * D], T.hs[:, f * n:(f + 1) * n],
+                pe.matmul(T.pc[:, 0:n], T.w2s[:, f * D:(f + 1) * D], hid[gi % 2][:, f * n:(f + 1) * n],
                           f == 0, f == FF - 1).then_inc(S.mm, 1)
-        for pi, (lo, hi, q) in enumerate(PIECES):
-            eng = v if q == "v" else sc
-            eng.wait_ge(S["m%d" % pi], (hi - lo) * (gi + 1))
-            if gi > 0:
-                eng.wait_ge(S.cp, gi)
-            w = (hi - lo) * n
-            if q == "v":
-                v.tensor_scalar(T.hs[:, lo * n:hi * n], banks[pi][:, 0:w], 0.0, None,
-                                AluOpType.max).then_inc(S["r%d" % pi], 1)
-            else:
-                sc.activation(T.hs[:, lo * n:hi * n], banks[pi][:, 0:w],
-                              ActivationFunctionType.Relu).then_inc(S["r%d" % pi], 1)
         v.wait_ge(S.mm, FF * (gi + 1))
         v.tensor_copy(out, T.pc[:, 0:n]).then_inc(S.cp, 1)
+
+    layer1(0)
+    for gi in range(len(groups)):
+        if gi + 1 < len(groups):
+            layer1(gi + 1)
+        layer2(gi)
 
 
 def rank_program(g, core, T, topo):
     cores = list(T.cores)
     S = T.sem
     rank = T.rank_of(core)
-    helpers = [_helper(topo, cores, m) for m in cores] if HELP_GROUPS else [None] * NR
-    main_steps = [j for G in MAIN_GROUPS for j in G]
-    help_steps = [j for G in HELP_GROUPS for j in G]
+    team = [_team(topo, cores, m) for m in cores]
+    NT = len(PLAN)
+
+    def place(j):
+        for i, P in enumerate(PLAN):
+            steps = [s_ for G in P for s_ in G]
+            if j in steps:
+                return i, steps.index(j) * CAP
+        return None
 
     def owner(e, j):
-        return cores[e] if j in main_steps else helpers[e]
+        return team[e][place(j)[0]]
 
     def landcol(j):
-        lst = main_steps if j in main_steps else help_steps
-        return lst.index(j) * CAP
+        return place(j)[1]
 
     def arrive(e, j):
         r = (e - j) % NR
@@ -156,17 +182,49 @@ def rank_program(g, core, T, topo):
                             T.outb[:, landcol(j):landcol(j) + CAP], S.back) for j in G], S.sent)
         return sent
 
-    def pass_mask(e, early):
-        far = topo.mask(cores[e], cores[(e + 1) % NR])
-        return topo.mask(cores[e], helpers[e]) & (far if early else ~far)
+    def link_mask(e, i, side):
+        m = topo.mask(team[e][i], team[e][i + 1])
+        if i == 0:
+            far = topo.mask(cores[e], cores[(e + 1) % NR])
+            m &= far if side == "far" else ~far
+        return m
+
+    def pass_on(e, i, when, have, sent):
+        rid, pid = topo.addr(team[e][i + 1], core)
+        for l, lo, hi, s_, q, early, side in CHUNKS:
+            if when is not None and early != when:
+                continue
+            buf = T.w1s if l == 1 else T.w2s
+            fm = link_mask(e, i, side)
+            g.wait_ge(S[s_], have(side))
+            g.remote_dma(out_ap=buf[:, lo * D:hi * D], in_ap=buf[:, lo * D:hi * D], remote_sem=S[s_],
+                         local_sem=S.sent, pid=pid, routing_id=rid, dma_engine_mask=fm)
+            sent += len(_bits(fm))
+        return sent
+
+    def zeros_count(e):
+        return _split(topo.mask(team[e][NT - 1], cores[e]), NR)[1] * NR
 
     if rank is None:
-        if core not in helpers:
+        mine = [(e, t.index(core)) for e, t in enumerate(team) if core in t]
+        if not mine:
             return
-        e = helpers.index(core)
-        wneed = dict(((l, lo), (S[s_], len(_bits(pass_mask(e, early))))) for l, lo, hi, s_, q, early in CHUNKS)
-        _expert(g, T, remote_groups(e, HELP_GROUPS), wneed)
-        g.wait_ge(S.sent, give_back(e, HELP_GROUPS, 0, 0))
+        e, i = mine[0]
+
+        def have(side):
+            return len(_bits(link_mask(e, i - 1, side)))
+
+        sent = 0
+        if i + 1 < NT:
+            sent = pass_on(e, i, None, have, sent)
+        else:
+            g.vector.memset(T.zb[:], 0.0).then_inc(S.ms, 1)
+            g.wait_ge(S.ms, 1)
+            sent += _post(g, topo, core, [(cores[e], T.res[:, b * STR + CAP:(b + 1) * STR], T.zb[:], S.zs)
+                                          for b in range(NR)], S.sent)
+        wneed = dict(((l, lo), (S[s_], have(side))) for l, lo, hi, s_, q, early, side in CHUNKS)
+        _expert(g, T, remote_groups(e, PLAN[i]), wneed)
+        g.wait_ge(S.sent, give_back(e, PLAN[i], 0, sent))
         return
 
     k = rank
@@ -175,7 +233,7 @@ def rank_program(g, core, T, topo):
     sy.dma_start(T.exi[:, 0:16], T.ex[:]).then_inc(S.idx, 16)
     sc.dma_start(T.exi[:, 16:32], T.pos[:]).then_inc(S.idx, 16)
     sy.dma_start(T.xs[:], T.x[:]).then_inc(S.xl, 16)
-    for l, lo, hi, s_, q, early in CHUNKS:
+    for l, lo, hi, s_, q, early, side in CHUNKS:
         buf, src = (T.w1s, T.w1) if l == 1 else (T.w2s, T.w2)
         (sc if q == "s" else sy).dma_start(buf[:, lo * D:hi * D], src[:, lo * D:hi * D]).then_inc(S[s_], 16)
 
@@ -199,27 +257,13 @@ def rank_program(g, core, T, topo):
     v.wait_ge(S.xl, 16)
     v.wait_ge(S.ms, NR)
     v.tensor_copy(T.send[:, 0:WIN].indirect(T.off[:, 0:16]), T.xs[:]).then_inc(S.sc, 1)
-    for e in range(NR):
-        v.memset(T.res[:, e * STR + CAP:(e + 1) * STR], 0.0).then_inc(S.zs, 1)
 
     sent = 0
 
-    def pass_on(when, sent):
-        if not HELP_GROUPS:
-            return sent
-        rid, pid = topo.addr(helpers[k], core)
-        for l, lo, hi, s_, q, early in CHUNKS:
-            if early != when:
-                continue
-            buf = T.w1s if l == 1 else T.w2s
-            fm = pass_mask(k, early)
-            g.wait_ge(S[s_], 16)
-            g.remote_dma(out_ap=buf[:, lo * D:hi * D], in_ap=buf[:, lo * D:hi * D], remote_sem=S[s_],
-                         local_sem=S.sent, pid=pid, routing_id=rid, dma_engine_mask=fm)
-            sent += len(_bits(fm))
-        return sent
+    def loaded(side):
+        return 16
 
-    sent = pass_on(True, sent)
+    sent = pass_on(k, 0, True, loaded, sent)
 
     g.wait_ge(S.sc, 1)
     for call in DISPATCH:
@@ -228,22 +272,22 @@ def rank_program(g, core, T, topo):
                         T.send[:, ((k + j) % NR) * STR:((k + j) % NR) * STR + CAP], S["a%d" % j]) for j in call],
                       S.sent)
 
-    sent = pass_on(False, sent)
+    sent = pass_on(k, 0, False, loaded, sent)
 
     own = (T.send[:, k * STR:k * STR + CAP], CAP, [(S.sc, 1)], T.res[:, k * STR:k * STR + CAP])
-    groups = [own] + remote_groups(k, MAIN_GROUPS)
-    _expert(g, T, groups, dict(((l, lo), (S[s_], 16)) for l, lo, hi, s_, q, early in CHUNKS))
-    sent = give_back(k, MAIN_GROUPS, 1, sent)
+    groups = [own] + remote_groups(k, PLAN[0])
+    _expert(g, T, groups, dict(((l, lo), (S[s_], 16)) for l, lo, hi, s_, q, early, side in CHUNKS))
+    sent = give_back(k, PLAN[0], 1, sent)
     g.wait_ge(S.sent, sent)
 
     back = 0
     for j in range(1, NR):
         e = (k + j) % NR
-        G = [G for G in MAIN_GROUPS + HELP_GROUPS if j in G][0]
+        G = [G for P in PLAN for G in P if j in G][0]
         back += _split(_common(topo, owner(e, j), [cores[(e - jj) % NR] for jj in G]), len(G))[1]
     for eng in (v, sc):
         eng.wait_ge(S.back, back)
-        eng.wait_ge(S.zs, NR)
+        eng.wait_ge(S.zs, zeros_count(k))
         eng.wait_ge(S.cp, len(groups))
         eng.wait_ge(S.cv, 2)
     h2 = TOK // 2

from concourse.bass import DstId, RemoteDMATransfer
from concourse.mybir import AluOpType, ActivationFunctionType

NR, TOK, CAP, FF, D = 8, 256, 48, 8, 128
STR = TOK
WIN = NR * STR
NSIM = 256

PLAN = [[[1, 2], [5]], [[3, 4], [6]], [[7]]]
DISPATCH = [[1, 2], [3, 4], [5], [6], [7]]
PIECES = [(0, 3, "v"), (3, 6, "s"), (6, 8, "v")]
GMAX = 2
CHUNKS = [(1, 0, 1, "w0", "s", True, "far"), (1, 1, 4, "wa", "s", False, "near"), (1, 4, 8, "wb", "y", False, "near"),
          (2, 0, 4, "wc", "s", False, "far"), (2, 4, 6, "wd", "y", False, "near"), (2, 6, 8, "we", "y", False, "near")]

SCRATCH = {
    "xs": ("sbuf", [128, TOK], "bfloat16"),
    "exi": ("sbuf", [16, 32], "int32"),
    "exb": ("sbuf", [16, 32], "bfloat16"),
    "rsel": ("sbuf", [16, 256], "bfloat16"),
    "off": ("sbuf", [128, 16], "uint16"),
    "send": ("sbuf", [128, WIN], "bfloat16"),
    "res": ("sbuf", [128, WIN], "bfloat16"),
    "land": ("sbuf", [128, (NR - 1) * CAP], "bfloat16"),
    "outb": ("sbuf", [128, (NR - 1) * CAP], "bfloat16"),
    "hs": ("sbuf", [128, FF * GMAX * CAP], "bfloat16"),
    "hs2": ("sbuf", [128, FF * GMAX * CAP], "bfloat16"),
    "w1s": ("sbuf", [128, FF * D], "bfloat16"),
    "w2s": ("sbuf", [128, FF * D], "bfloat16"),
    "ys": ("sbuf", [128, TOK], "bfloat16"),
    "zb": ("sbuf", [128, STR - CAP], "bfloat16"),
    "p0": ("psum", [128, 512], "float32"),
    "p1": ("psum", [128, 512], "float32"),
    "p2": ("psum", [128, 512], "float32"),
    "q0": ("psum", [128, 512], "float32"),
    "q1": ("psum", [128, 512], "float32"),
    "q2": ("psum", [128, 512], "float32"),
    "pc": ("psum", [128, 512], "float32"),
    "po": ("psum", [128, 512], "float32"),
}
SEMAPHORES = ["idx", "xl", "w0", "wa", "wb", "wc", "wd", "we", "rm", "ms", "zs", "cv", "of", "rs", "sc",
              "a1", "a2", "a3", "a4", "a5", "a6", "a7", "m0", "m1", "m2", "r0", "r1", "r2",
              "n0", "n1", "n2", "u0", "u1", "u2", "mm", "cp", "sent", "back", "g1", "g2", "st"]


def _bits(mask):
    return [1 << b for b in range(16) if (mask >> b) & 1]


def _split(mask, n):
    e = _bits(mask)
    per = 1
    while per * 2 * n <= len(e):
        per *= 2
    return [sum(e[i * per:(i + 1) * per]) for i in range(n)], per


def _common(topo, src, dsts):
    m = topo.mask(src, dsts[0])
    for d in dsts[1:]:
        m &= topo.mask(src, d)
    return m


def _post(g, topo, src, items, local_sem):
    subs, per = _split(_common(topo, src, [it[0] for it in items]), len(items))
    if len(items) == 1:
        d, o, i_, s = items[0]
        rid, pid = topo.addr(d, src)
        g.remote_dma(out_ap=o, in_ap=i_, remote_sem=s, local_sem=local_sem, pid=pid, routing_id=rid,
                     dma_engine_mask=subs[0])
    else:
        tr = []
        for (d, o, i_, s), m in zip(items, subs):
            rid, pid = topo.addr(d, src)
            tr.append(RemoteDMATransfer(dst_ids=[DstId(rid=rid, pnc=pid)], dma_engine_mask=m, remote_sem=s,
                                        src=i_, dst=o))
        g.remote_dma_fused(tr, local_sem=local_sem)
    return per * len(items)


def _team(topo, cores, m):
    more = [c for c in range(NSIM)
            if (c not in cores and topo.host(c) == topo.host(m) and topo.chip(c) == topo.chip(m)
                and topo.die(c) == topo.die(m) and all(topo.may_write(c, d) for d in cores))]
    return [m] + more[:len(PLAN) - 1]


def _expert(g, T, groups, wneed):
    S = T.sem
    pe, v, sc = g.tensor, g.vector, g.scalar
    banks = [[T.p0, T.p1, T.p2], [T.q0, T.q1, T.q2]]
    hid = [T.hs, T.hs2]

    def msem(gi, pi):
        return S["%s%d" % ("mn"[gi % 2], pi)]

    def rsem(gi, pi):
        return S["%s%d" % ("ru"[gi % 2], pi)]

    def layer1(gi):
        rhs, n, waits, out = groups[gi]
        for s_, val in waits:
            pe.wait_ge(s_, val)
        for pi, (lo, hi, q) in enumerate(PIECES):
            for f in range(lo, hi):
                if gi == 0 and (1, f) in wneed:
                    pe.wait_ge(*wneed[(1, f)])
                pe.matmul(banks[gi % 2][pi][:, (f - lo) * n:(f - lo + 1) * n], T.w1s[:, f * D:(f + 1) * D], rhs,
                          True, True).then_inc(msem(gi, pi), 1)
        for pi, (lo, hi, q) in enumerate(PIECES):
            eng = v if q == "v" else sc
            eng.wait_ge(msem(gi, pi), (hi - lo) * (gi // 2 + 1))
            if gi > 1:
                eng.wait_ge(S.cp, gi - 1)
            w = (hi - lo) * n
            if q == "v":
                v.tensor_scalar(hid[gi % 2][:, lo * n:hi * n], banks[gi % 2][pi][:, 0:w], 0.0, None,
                                AluOpType.max).then_inc(rsem(gi, pi), 1)
            else:
                sc.activation(hid[gi % 2][:, lo * n:hi * n], banks[gi % 2][pi][:, 0:w],
                              ActivationFunctionType.Relu).then_inc(rsem(gi, pi), 1)

    def layer2(gi):
        rhs, n, waits, out = groups[gi]
        if gi > 0:
            pe.wait_ge(S.cp, gi)
        for pi, (lo, hi, q) in enumerate(PIECES):
            pe.wait_ge(rsem(gi, pi), gi // 2 + 1)
            for f in range(lo, hi):
                if gi == 0 and (2, f) in wneed:
                    pe.wait_ge(*wneed[(2, f)])
                pe.matmul(T.pc[:, 0:n], T.w2s[:, f * D:(f + 1) * D], hid[gi % 2][:, f * n:(f + 1) * n],
                          f == 0, f == FF - 1).then_inc(S.mm, 1)
        v.wait_ge(S.mm, FF * (gi + 1))
        v.tensor_copy(out, T.pc[:, 0:n]).then_inc(S.cp, 1)

    layer1(0)
    for gi in range(len(groups)):
        if gi + 1 < len(groups):
            layer1(gi + 1)
        layer2(gi)


def rank_program(g, core, T, topo):
    cores = list(T.cores)
    S = T.sem
    rank = T.rank_of(core)
    team = [_team(topo, cores, m) for m in cores]
    NT = len(PLAN)

    def place(j):
        for i, P in enumerate(PLAN):
            steps = [s_ for G in P for s_ in G]
            if j in steps:
                return i, steps.index(j) * CAP
        return None

    def owner(e, j):
        return team[e][place(j)[0]]

    def landcol(j):
        return place(j)[1]

    def arrive(e, j):
        r = (e - j) % NR
        call = [c for c in DISPATCH if j in c][0]
        return _split(_common(topo, cores[r], [owner((r + jj) % NR, jj) for jj in call]), len(call))[1]

    def remote_groups(e, plan):
        out = []
        for G in plan:
            c0, n = landcol(G[0]), CAP * len(G)
            out.append((T.land[:, c0:c0 + n], n, [(S["a%d" % j], arrive(e, j)) for j in G], T.outb[:, c0:c0 + n]))
        return out

    def give_back(e, plan, first, sent):
        for i, G in enumerate(plan):
            g.wait_ge(S.cp, first + i + 1)
            sent += _post(g, topo, core,
                          [(cores[(e - j) % NR], T.res[:, e * STR:e * STR + CAP],
                            T.outb[:, landcol(j):landcol(j) + CAP], S.back) for j in G], S.sent)
        return sent

    def link_mask(e, i, side):
        m = topo.mask(team[e][i], team[e][i + 1])
        if i == 0:
            far = topo.mask(cores[e], cores[(e + 1) % NR])
            m &= far if side == "far" else ~far
        return m

    def pass_on(e, i, when, have, sent):
        rid, pid = topo.addr(team[e][i + 1], core)
        for l, lo, hi, s_, q, early, side in CHUNKS:
            if when is not None and early != when:
                continue
            buf = T.w1s if l == 1 else T.w2s
            fm = link_mask(e, i, side)
            g.wait_ge(S[s_], have(side))
            g.remote_dma(out_ap=buf[:, lo * D:hi * D], in_ap=buf[:, lo * D:hi * D], remote_sem=S[s_],
                         local_sem=S.sent, pid=pid, routing_id=rid, dma_engine_mask=fm)
            sent += len(_bits(fm))
        return sent

    def zeros_count(e):
        return _split(topo.mask(team[e][NT - 1], cores[e]), NR)[1] * NR

    if rank is None:
        mine = [(e, t.index(core)) for e, t in enumerate(team) if core in t]
        if not mine:
            return
        e, i = mine[0]

        def have(side):
            return len(_bits(link_mask(e, i - 1, side)))

        sent = 0
        if i + 1 < NT:
            sent = pass_on(e, i, None, have, sent)
        else:
            g.vector.memset(T.zb[:], 0.0).then_inc(S.ms, 1)
            g.wait_ge(S.ms, 1)
            sent += _post(g, topo, core, [(cores[e], T.res[:, b * STR + CAP:(b + 1) * STR], T.zb[:], S.zs)
                                          for b in range(NR)], S.sent)
        wneed = dict(((l, lo), (S[s_], have(side))) for l, lo, hi, s_, q, early, side in CHUNKS)
        _expert(g, T, remote_groups(e, PLAN[i]), wneed)
        g.wait_ge(S.sent, give_back(e, PLAN[i], 0, sent))
        return

    k = rank
    v, sc, pe, sy = g.vector, g.scalar, g.tensor, g.sync

    sy.dma_start(T.exi[:, 0:16], T.ex[:]).then_inc(S.idx, 16)
    sc.dma_start(T.exi[:, 16:32], T.pos[:]).then_inc(S.idx, 16)
    sy.dma_start(T.xs[:], T.x[:]).then_inc(S.xl, 16)
    for l, lo, hi, s_, q, early, side in CHUNKS:
        buf, src = (T.w1s, T.w1) if l == 1 else (T.w2s, T.w2)
        (sc if q == "s" else sy).dma_start(buf[:, lo * D:hi * D], src[:, lo * D:hi * D]).then_inc(S[s_], 16)

    v.memset(T.rsel[:, 0:128], float(STR)).then_inc(S.rm, 1)
    v.memset(T.rsel[:, 128:256], 1.0).then_inc(S.rm, 1)
    for e in range(NR):
        v.memset(T.send[:, e * STR:e * STR + CAP], 0.0).then_inc(S.ms, 1)
    g.wait_ge(S.rm, 2)
    g.affine_select(T.rsel[:], T.rsel[:], [[0, 16], [-1, 16]], AluOpType.is_equal, 0.0, 0, 1).then_inc(S.rs, 1)

    v.wait_ge(S.idx, 32)
    v.tensor_copy(T.exb[:], T.exi[:]).then_inc(S.cv, 1)
    pe.wait_ge(S.cv, 1)
    pe.wait_ge(S.rs, 1)
    pe.matmul(T.po[:, 0:16], T.rsel[:, 0:128], T.exb[:, 0:16], True, False).then_inc(S.of, 1)
    pe.matmul(T.po[:, 0:16], T.rsel[:, 128:256], T.exb[:, 16:32], False, True).then_inc(S.of, 1)
    v.wait_ge(S.of, 2)
    v.tensor_copy(T.off[:], T.po[:, 0:16]).then_inc(S.cv, 1)

    v.wait_ge(S.cv, 2)
    v.wait_ge(S.xl, 16)
    v.wait_ge(S.ms, NR)
    v.tensor_copy(T.send[:, 0:WIN].indirect(T.off[:, 0:16]), T.xs[:]).then_inc(S.sc, 1)

    sent = 0

    def loaded(side):
        return 16

    sent = pass_on(k, 0, True, loaded, sent)

    g.wait_ge(S.sc, 1)
    for call in DISPATCH:
        sent += _post(g, topo, core,
                      [(owner((k + j) % NR, j), T.land[:, landcol(j):landcol(j) + CAP],
                        T.send[:, ((k + j) % NR) * STR:((k + j) % NR) * STR + CAP], S["a%d" % j]) for j in call],
                      S.sent)

    sent = pass_on(k, 0, False, loaded, sent)

    own = (T.send[:, k * STR:k * STR + CAP], CAP, [(S.sc, 1)], T.res[:, k * STR:k * STR + CAP])
    groups = [own] + remote_groups(k, PLAN[0])
    _expert(g, T, groups, dict(((l, lo), (S[s_], 16)) for l, lo, hi, s_, q, early, side in CHUNKS))
    sent = give_back(k, PLAN[0], 1, sent)
    g.wait_ge(S.sent, sent)

    back = 0
    for j in range(1, NR):
        e = (k + j) % NR
        G = [G for P in PLAN for G in P if j in G][0]
        back += _split(_common(topo, owner(e, j), [cores[(e - jj) % NR] for jj in G]), len(G))[1]
    for eng in (v, sc):
        eng.wait_ge(S.back, back)
        eng.wait_ge(S.zs, zeros_count(k))
        eng.wait_ge(S.cp, len(groups))
        eng.wait_ge(S.cv, 2)
    h2 = TOK // 2
    v.tensor_copy(T.ys[:, 0:h2], T.res[:, 0:WIN].indirect(T.off[:, 0:8])).then_inc(S.g1, 1)
    sc.activation(T.ys[:, h2:TOK], T.res[:, 0:WIN].indirect(T.off[:, 8:16]),
                  ActivationFunctionType.Copy).then_inc(S.g2, 1)
    sy.wait_ge(S.g1, 1)
    sy.dma_start(T.y[:, 0:h2], T.ys[:, 0:h2]).then_inc(S.st, 16)
    sc.wait_ge(S.g2, 1)
    sc.dma_start(T.y[:, h2:TOK], T.ys[:, h2:TOK]).then_inc(S.st, 16)
    sy.wait_ge(S.st, 32)
